import numpy as np
import ml_dtypes


def mxq(x, axis, fmt="e4m3"):
    dtype, down = {"e4m3": (ml_dtypes.float8_e4m3fn, 7), "e5m2": (ml_dtypes.float8_e5m2, 14)}[fmt]
    v = np.moveaxis(np.asarray(x, np.float32).astype(ml_dtypes.bfloat16).astype(np.float64), axis, -1)
    blocks = v.reshape(v.shape[:-1] + (-1, 32))
    amax = np.abs(blocks).max(-1, keepdims=True)
    byte = np.maximum(np.where(amax > 0, np.frexp(amax)[1] - 1 + 127, 0) - down, 1)
    scale = np.exp2(byte - 127.0)
    codes = (blocks / scale).astype(np.float32).astype(dtype).astype(np.float64)
    return np.moveaxis((codes * scale).reshape(v.shape), -1, axis)


WIDE = False


def mx_kscale(k):
    if not WIDE:
        return np.ones(k)
    levels = np.array([10, -10, 5, -5, 0])
    if k % 512:
        return np.exp2(np.random.permutation(np.resize(levels, k // 32))).repeat(32)
    a = np.empty((k // 512, 16))
    for p in range(k // 512):
        a[p, :8] = np.random.permutation(np.resize(levels, 8))
        for g in range(8):
            far = levels[np.abs(levels - a[p, g]) >= 10]
            a[p, g + 8] = far[np.random.randint(len(far))]
    return np.exp2(a.ravel()).repeat(32)


def f64(x):
    return np.asarray(x).astype(np.float64)


def striped(idx):
    return np.tile(idx.reshape(-1, 16).T, (8, 1)).astype(np.uint16)


def unstriped(offs):
    return offs[:16].T.reshape(-1).astype(np.int64)


E2M1 = np.array([0.0, 0.5, 1.0, 1.5, 2.0, 3.0, 4.0, 6.0, -0.0, -0.5, -1.0, -1.5, -2.0, -3.0, -4.0, -6.0])


def pack_fp4(w):
    k, n = w.shape
    w = f64(np.asarray(w, np.float32).astype(ml_dtypes.bfloat16)).reshape(k // 32, 32, n)
    amax = np.abs(w).max(1)
    mant, ex = np.frexp(amax / 6.0)
    byte = np.clip(np.where(amax > 0, np.where(mant > 0.5, ex, ex - 1) + 127, 1), 1, 254)
    scaled = (w * np.exp2(127.0 - byte)[:, None, :]).reshape(k, n).astype(np.float32)
    c = np.ascontiguousarray(scaled.reshape(k // 512, 128, 4, n).transpose(0, 1, 3, 2)).astype(ml_dtypes.float4_e2m1fn).view(np.uint8) & 0xF
    words = (c[..., 0::2] | (c[..., 1::2] << 4)).reshape(k // 512, 128, 2 * n)
    return np.ascontiguousarray(words), np.ascontiguousarray(byte.astype(np.uint8).reshape(k // 512, 16, n))


def unpack_fp4(words, scales):
    g, _, n = scales.shape
    words = np.ascontiguousarray(words).reshape(g, 128, n, 2)
    nib = np.empty((g, 128, n, 4), np.uint8)
    nib[..., 0::2] = words & 0xF
    nib[..., 1::2] = words >> 4
    vals = E2M1[nib] * np.repeat(np.exp2(scales.astype(np.float64) - 127.0), 8, axis=1)[..., None]
    return vals.transpose(0, 1, 3, 2).reshape(g * 512, n)


def silu(v):
    return v / (1.0 + np.exp(-np.maximum(v, -700.0)))


K, T, S, N = 512, 2048, 1024, 128
P = 2 ** 7


def setup_inputs():
    n = np.random.standard_normal
    s = mx_kscale(K)[:, None]
    packed_w1 = pack_fp4(n((K, N)) / np.sqrt(K) / s)
    return {
        "xT": (n((K, T)) * s).astype(np.float32),
        "mean": np.tile(0.3 * np.random.standard_normal(T), (P, 1)).astype(np.float32),
        "inv": np.tile(np.random.uniform(0.5, 2.0, T), (P, 1)).astype(np.float32),
        "gsum": n((N, 1)).astype(np.float32),
        "b": (0.3 * n((N, 1))).astype(np.float32),
        "w1_words": packed_w1[0],
        "w1_scales": packed_w1[1],
        "offs": striped(np.random.permutation(T)[:S]),
    }


def reference(xT, mean, inv, gsum, b, w1_words, w1_scales, offs):
    xq = mxq(f64(xT)[:, unstriped(offs)], 0, "e4m3")
    y = unpack_fp4(w1_words, w1_scales).T @ xq
    mg = f64(mean)[:1][:, unstriped(offs)]
    ig = f64(inv)[:1][:, unstriped(offs)]
    return silu((y - (f64(gsum) * mg)) * ig + f64(b))

@@ -1,0 +1,180 @@
+from contextlib import ExitStack
+
+import concourse.mybir as mybir
+from concourse.masks import make_identity
+
+K, T, S, N = 512, 2048, 1024, 128
+P = 128
+FLOPS = 2 * K * S * N
+
+F32 = mybir.dt.float32
+BF16 = mybir.dt.bfloat16
+I32 = mybir.dt.int32
+U32 = mybir.dt.uint32
+U16 = mybir.dt.uint16
+U8 = mybir.dt.uint8
+FP8X4 = mybir.dt.float8_e4m3fn_x4
+FP4X4 = mybir.dt.float4_e2m1fn_x4
+ACT = mybir.ActivationFunctionType
+ALU = mybir.AluOpType
+
+CHUNK = 256
+BLOCKS = S // P
+LOADS = [[0,0,512,0],[0,512,512,0],[0,1024,512,512],[0,1536,512,512],[1,0,512,0],[1,512,512,0],[1,1024,512,0],[1,1536,512,352]]
+UNITS = [[0,2,False,"a"],[2,2,False,"b"],[4,2,False,"a"],[6,1,True,"b"],[7,1,True,"g"]]
+
+
+def tile_picked_lnfold_silu_l_kernel(
+    tc, xT, mean, inv, gsum, b, w1_words, w1_scales, offs, out
+):
+    nc = tc.nc
+    with ExitStack() as ctx:
+        keep = ctx.enter_context(tc.tile_pool(name="keep", bufs=1))
+        psum = ctx.enter_context(tc.psum_pool(name="psum", bufs=1))
+
+        offsets = keep.tile([P, S // 16], U16, name="offsets")
+        stat_rows = keep.tile([2, T], F32, name="stat_rows")
+        nc.sync.dma_start(out=stat_rows[0:1, :], in_=mean[0:1, :])
+        nc.sync.dma_start(out=stat_rows[1:2, :], in_=inv[0:1, :])
+        stats = keep.tile([P, T], F32, name="stats", tag="window_then_picked", align_bytes=64)
+        nc.vector.memset(stats[:], 0.0)
+        warm = keep.tile([P, 2], F32, name="warm")
+        nc.gpsimd.memset(warm[:, 0:1], 0.0)
+        nc.scalar.activation(out=warm[:, 1:2], in_=warm[:, 0:1], func=ACT.Silu)
+        w_scales = keep.tile([P, N], U8, name="w_scales", align_bytes=64)
+        nc.gpsimd.memset(w_scales[:], 0)
+        ident = keep.tile([P, P], F32, name="ident")
+        make_identity(nc, ident[:])
+
+        rows = xT.rearrange("(p j) t -> p j t", j=4)
+        pairs = [keep.tile([P, 2 * T], BF16, name="pairs%d" % u, align_bytes=64) for u in range(2)]
+        raws = [keep.tile([P, 2, w], F32, name="raw%d" % i, tag="raw%d" % i) for i, (u, c0, w, v) in enumerate(LOADS)]
+        gsum_col = keep.tile([P, 1], F32, name="gsum_col")
+        b_col = keep.tile([P, 1], F32, name="b_col")
+        w_words = keep.tile([P, 2 * N], U8, name="w_words", align_bytes=64)
+
+        def load(i):
+            u, c0, w, v = LOADS[i]
+            nc.sync.dma_start(out=raws[i][:], in_=rows[:, 2 * u : 2 * u + 2, c0 : c0 + w])
+
+        def cast(i):
+            u, c0, w, v = LOADS[i]
+            dst = pairs[u][:, 2 * c0 : 2 * (c0 + w)].rearrange("p (t e) -> p t e", e=2)
+            src = raws[i][:].rearrange("p e t -> p t e")
+            if v > 0:
+                nc.vector.tensor_copy(out=dst[:, 0:v, :], in_=src[:, 0:v, :])
+            if v < w:
+                nc.scalar.copy(out=dst[:, v:w, :], in_=src[:, v:w, :])
+
+        load(0)
+        nc.sync.dma_start(offsets[:], offs)
+        nc.sync.dma_start(out=gsum_col[:], in_=gsum)
+        for i in range(1, len(LOADS)):
+            load(i)
+        nc.sync.dma_start(out=w_words[:], in_=w1_words[0])
+        for q in range(4):
+            nc.sync.dma_start(
+                out=w_scales[32 * q : 32 * q + 4, :].bitcast(I32),
+                in_=w1_scales[0, 4 * q : 4 * q + 4, :].bitcast(I32),
+            )
+        nc.sync.dma_start(out=b_col[:], in_=b)
+
+        gsum_turned = psum.tile([P, P], F32, name="gsum_turned", tag="g")
+        nc.tensor.transpose(gsum_turned[:], gsum_col[:].to_broadcast([P, P]), ident[:])
+        gsum_row = keep.tile([P, P], F32, name="gsum_row")
+        nc.scalar.activation(out=gsum_row[:], in_=gsum_turned[:], func=ACT.Copy, scale=-1.0)
+        nc.vector.tensor_copy(out=stats[0:2, :], in_=stat_rows[:])
+        picked_stats = keep.tile([P, S], F32, name="picked_stats")
+        nc.vector.tensor_copy(out=picked_stats[:], in_=stats[:].indirect(offsets[:]))
+        for i in range(len(LOADS)):
+            if LOADS[i][0] == 0:
+                cast(i)
+
+        chunks = S // CHUNK
+        picked = keep.tile([P, 4 * S], BF16, name="picked", tag="window_then_picked", align_bytes=64)
+
+        def gather(u, c, width):
+            dst = picked[:, 4 * c : 4 * (c + width)].bitcast(U32).rearrange("p (j u) -> p j u", u=2)
+            cols = slice(c // 16, (c + width) // 16)
+            nc.vector.tensor_copy(out=dst[:, :, u], in_=pairs[u][:].bitcast(U32).indirect(offsets[:, cols]))
+
+        for c in range(0, S, 1024):
+            gather(0, c, 1024)
+        for i in range(len(LOADS)):
+            if LOADS[i][0] == 1:
+                cast(i)
+
+        token_stats = keep.tile([P, BLOCKS, 2], F32, name="token_stats", tag="raw%d" % (len(LOADS) - 2))
+        for h in range(2):
+            turned = psum.tile([P, 4, P], F32, name="turned%d" % h, tag="ab"[h])
+            for i in range(4):
+                blk = 4 * h + i
+                nc.tensor.transpose(turned[:, i, :], picked_stats[:, blk * P : (blk + 1) * P], ident[:])
+            nc.scalar.copy(out=token_stats[:, 4 * h : 4 * h + 4, :], in_=turned[:, :, 0:2])
+        shift = keep.tile([P, BLOCKS], F32, name="shift")
+        nc.gpsimd.tensor_tensor(out=shift[:], in0=token_stats[:, :, 0], in1=token_stats[:, :, 1], op=ALU.mult)
+        correction = keep.tile([P, BLOCKS, N], F32, name="correction", tag="raw%d" % (len(LOADS) - 1))
+        for blk in range(BLOCKS):
+            nc.scalar.activation(
+                out=correction[:, blk, :], in_=gsum_row[:], func=ACT.Copy, scale=shift[:, blk : blk + 1]
+            )
+        zs = []
+        for n, (first, count, on_vector, bank) in enumerate(UNITS):
+            zs.append(psum.tile([P, count, P], F32, name="z%d" % n))
+            if not on_vector:
+                for i in range(count):
+                    nc.tensor.matmul(
+                        zs[n][:, i, :], correction[:, first + i, :], ident[:],
+                        start=(i == 0), stop=False, is_transpose=True,
+                    )
+
+        results = []
+
+        def finish(n):
+            first, count, on_vector, bank = UNITS[n]
+            width = count * P
+            codes = keep.tile([P, width], U32, name="codes%d" % n, align_bytes=64)
+            scales = keep.tile([P, width], U8, name="scales%d" % n, align_bytes=64)
+            nc.vector.quantize_mx(
+                out=codes[:].bitcast(FP8X4), scales=scales[:],
+                in_=picked[:, 4 * first * P : 4 * (first * P + width)],
+            )
+            y = psum.tile([P, count, N], F32, name="y%d" % n, tag=bank)
+            z = zs[n]
+            scaled = keep.tile([P, count, N], F32, name="scaled%d" % n)
+            for i in range(count):
+                cols = slice(i * P, (i + 1) * P)
+                nc.tensor.matmul_mx(
+                    out=y[:, i, :], lhsT=codes[:, cols].bitcast(FP8X4), lhsT_scale=scales[:, cols],
+                    rhs=w_words[:].bitcast(FP4X4), rhs_scale=w_scales[:], start=True, stop=True,
+                )
+            for i in range(count):
+                blk = first + i
+                if on_vector:
+                    nc.vector.scalar_tensor_tensor(
+                        out=scaled[:, i, :], in0=y[:, i, :], scalar=token_stats[:, blk, 1:2],
+                        in1=correction[:, blk, :], op0=ALU.mult, op1=ALU.add,
+                    )
+                else:
+                    nc.scalar.activation(
+                        out=scaled[:, i, :], in_=y[:, i, :], func=ACT.Copy, scale=token_stats[:, blk, 1:2]
+                    )
+            for i in range(count):
+                nc.tensor.matmul(
+                    z[:, i, :], scaled[:, i, :], ident[:],
+                    start=on_vector, stop=(on_vector or i == count - 1), is_transpose=True,
+                )
+            result = keep.tile([P, count, P], F32, name="result%d" % n)
+            results.append(result)
+            nc.scalar.activation(out=result[:], in_=z[:], func=ACT.Silu, bias=b_col[:])
+            nc.sync.dma_start(
+                out=out[:, first * P : first * P + width], in_=result[:].rearrange("p i j -> p (i j)")
+            )
+
+        gather(1, 0, CHUNK)
+        for c in range(chunks):
+            if c + 1 < chunks:
+                gather(1, (c + 1) * CHUNK, CHUNK)
+            for n in range(len(UNITS)):
+                if UNITS[n][0] * P // CHUNK == c:
+                    finish(n)

@@ -20,7 +20,7 @@ ALU = mybir.AluOpType
 
 CHUNK = 256
 BLOCKS = S // P
-LOADS = [[0,0,512,0],[0,512,512,0],[0,1024,512,512],[0,1536,512,512],[1,0,512,0],[1,512,512,0],[1,1024,512,0],[1,1536,512,352]]
+LOADS = [[0,0,256,0],[0,256,768,0],[0,1024,1024,704],[1,0,512,0],[1,512,512,0],[1,1024,512,128],[1,1536,512,352]]
 UNITS = [[0,2,False,"a"],[2,2,False,"b"],[4,2,False,"a"],[6,1,True,"b"],[7,1,True,"g"]]
 
 
@@ -34,10 +34,8 @@ def tile_picked_lnfold_silu_l_kernel(
 
         offsets = keep.tile([P, S // 16], U16, name="offsets")
         stat_rows = keep.tile([2, T], F32, name="stat_rows")
-        nc.sync.dma_start(out=stat_rows[0:1, :], in_=mean[0:1, :])
-        nc.sync.dma_start(out=stat_rows[1:2, :], in_=inv[0:1, :])
         stats = keep.tile([P, T], F32, name="stats", tag="window_then_picked", align_bytes=64)
-        nc.vector.memset(stats[:], 0.0)
+        nc.vector.memset(stats[:].bitcast(I32), 0)
         warm = keep.tile([P, 2], F32, name="warm")
         nc.gpsimd.memset(warm[:, 0:1], 0.0)
         nc.scalar.activation(out=warm[:, 1:2], in_=warm[:, 0:1], func=ACT.Silu)
@@ -47,7 +45,7 @@ def tile_picked_lnfold_silu_l_kernel(
         make_identity(nc, ident[:])
 
         rows = xT.rearrange("(p j) t -> p j t", j=4)
-        pairs = [keep.tile([P, 2 * T], BF16, name="pairs%d" % u, align_bytes=64) for u in range(2)]
+        pairs = [keep.tile([P, 2 * T], BF16, name="pairs%d" % u, tag="pairs%d" % u, align_bytes=64) for u in range(2)]
         raws = [keep.tile([P, 2, w], F32, name="raw%d" % i, tag="raw%d" % i) for i, (u, c0, w, v) in enumerate(LOADS)]
         gsum_col = keep.tile([P, 1], F32, name="gsum_col")
         b_col = keep.tile([P, 1], F32, name="b_col")
@@ -67,6 +65,8 @@ def tile_picked_lnfold_silu_l_kernel(
                 nc.scalar.copy(out=dst[:, v:w, :], in_=src[:, v:w, :])
 
         load(0)
+        nc.sync.dma_start(out=stat_rows[0:1, :], in_=mean[0:1, :])
+        nc.sync.dma_start(out=stat_rows[1:2, :], in_=inv[0:1, :])
         nc.sync.dma_start(offsets[:], offs)
         nc.sync.dma_start(out=gsum_col[:], in_=gsum)
         for i in range(1, len(LOADS)):
@@ -100,19 +100,19 @@ def tile_picked_lnfold_silu_l_kernel(
 
         for c in range(0, S, 1024):
             gather(0, c, 1024)
-        for i in range(len(LOADS)):
-            if LOADS[i][0] == 1:
-                cast(i)
-
-        token_stats = keep.tile([P, BLOCKS, 2], F32, name="token_stats", tag="raw%d" % (len(LOADS) - 2))
+        token_stats = keep.tile([P, BLOCKS, 2], F32, name="token_stats", tag="pairs0", align_bytes=64)
         for h in range(2):
             turned = psum.tile([P, 4, P], F32, name="turned%d" % h, tag="ab"[h])
             for i in range(4):
                 blk = 4 * h + i
                 nc.tensor.transpose(turned[:, i, :], picked_stats[:, blk * P : (blk + 1) * P], ident[:])
-            nc.scalar.copy(out=token_stats[:, 4 * h : 4 * h + 4, :], in_=turned[:, :, 0:2])
+            nc.vector.tensor_copy(out=token_stats[:, 4 * h : 4 * h + 4, :], in_=turned[:, :, 0:2])
         shift = keep.tile([P, BLOCKS], F32, name="shift")
-        nc.gpsimd.tensor_tensor(out=shift[:], in0=token_stats[:, :, 0], in1=token_stats[:, :, 1], op=ALU.mult)
+        nc.vector.tensor_tensor(out=shift[:], in0=token_stats[:, :, 0], in1=token_stats[:, :, 1], op=ALU.mult)
+        for i in range(len(LOADS)):
+            if LOADS[i][0] == 1:
+                cast(i)
+
         correction = keep.tile([P, BLOCKS, N], F32, name="correction", tag="raw%d" % (len(LOADS) - 1))
         for blk in range(BLOCKS):
             nc.scalar.activation(
@@ -167,7 +167,8 @@ def tile_picked_lnfold_silu_l_kernel(
             result = keep.tile([P, count, P], F32, name="result%d" % n)
             results.append(result)
             nc.scalar.activation(out=result[:], in_=z[:], func=ACT.Silu, bias=b_col[:])
-            nc.sync.dma_start(
+            queue = nc.scalar if n == len(UNITS) - 1 else nc.sync
+            queue.dma_start(
                 out=out[:, first * P : first * P + width], in_=result[:].rearrange("p i j -> p (i j)")
             )
 

@@ -91,15 +91,21 @@ def tile_picked_lnfold_silu_l_kernel(
                 cast(i)
 
         chunks = S // CHUNK
-        picked = keep.tile([P, 4 * S], BF16, name="picked", tag="window_then_picked", align_bytes=64)
+        picks = keep.tile([P, 2 * S], U32, name="picks", tag="window_then_picked", align_bytes=64)
+        woven = [keep.tile([P, 2 * CHUNK], U32, name="woven%d" % c, align_bytes=64) for c in range(chunks)]
 
         def gather(u, c, width):
-            dst = picked[:, 4 * c : 4 * (c + width)].bitcast(U32).rearrange("p (j u) -> p j u", u=2)
             cols = slice(c // 16, (c + width) // 16)
-            nc.vector.tensor_copy(out=dst[:, :, u], in_=pairs[u][:].bitcast(U32).indirect(offsets[:, cols]))
+            nc.vector.tensor_copy(
+                out=picks[:, u * S + c : u * S + c + width], in_=pairs[u][:].bitcast(U32).indirect(offsets[:, cols])
+            )
 
-        for c in range(0, S, 1024):
-            gather(0, c, 1024)
+        def weave(c):
+            dst = woven[c][:].rearrange("p (j u) -> p j u", u=2)
+            src = picks[:].rearrange("p (u j) -> p j u", u=2)[:, c * CHUNK : (c + 1) * CHUNK, :]
+            nc.vector.tensor_copy(out=dst.bitcast(I32), in_=src.bitcast(I32))
+
+        gather(0, 0, S)
         token_stats = keep.tile([P, BLOCKS, 2], F32, name="token_stats", tag="pairs0", align_bytes=64)
         for h in range(2):
             turned = psum.tile([P, 4, P], F32, name="turned%d" % h, tag="ab"[h])
@@ -137,7 +143,7 @@ def tile_picked_lnfold_silu_l_kernel(
             scales = keep.tile([P, width], U8, name="scales%d" % n, align_bytes=64)
             nc.vector.quantize_mx(
                 out=codes[:].bitcast(FP8X4), scales=scales[:],
-                in_=picked[:, 4 * first * P : 4 * (first * P + width)],
+                in_=woven[first * P // CHUNK][:, 2 * (first * P % CHUNK) : 2 * (first * P % CHUNK + width)].bitcast(BF16),
             )
             y = psum.tile([P, count, N], F32, name="y%d" % n, tag=bank)
             z = zs[n]
@@ -173,9 +179,15 @@ def tile_picked_lnfold_silu_l_kernel(
             )
 
         gather(1, 0, CHUNK)
-        for c in range(chunks):
-            if c + 1 < chunks:
-                gather(1, (c + 1) * CHUNK, CHUNK)
-            for n in range(len(UNITS)):
-                if UNITS[n][0] * P // CHUNK == c:
-                    finish(n)
+        gather(1, CHUNK, CHUNK)
+        weave(0)
+        gather(1, 2 * CHUNK, CHUNK)
+        finish(0)
+        weave(1)
+        gather(1, 3 * CHUNK, CHUNK)
+        finish(1)
+        weave(2)
+        weave(3)
+        finish(2)
+        finish(3)
+        finish(4)

@@ -18,10 +18,32 @@ FP4X4 = mybir.dt.float4_e2m1fn_x4
 ACT = mybir.ActivationFunctionType
 ALU = mybir.AluOpType
 
+LIST_COLUMN = 16
 CHUNK = 256
+CHUNKS = S // CHUNK
 BLOCKS = S // P
-LOADS = [[0,0,256,0],[0,256,768,0],[0,1024,1024,704],[1,0,512,0],[1,512,512,0],[1,1024,512,128],[1,1536,512,352]]
-UNITS = [[0,2,False,"a"],[2,2,False,"b"],[4,2,False,"a"],[6,1,True,"b"],[7,1,True,"g"]]
+BLOCKS_A_BANK = 4
+
+LOADS = [
+    (0, 0, 256, 0),
+    (0, 256, 768, 0),
+    (0, 1024, 1024, 704),
+    (1, 0, 512, 0),
+    (1, 512, 512, 0),
+    (1, 1024, 640, 640),
+    (1, 1664, 384, 384),
+]
+PAIR1_FIRST = 3
+
+GROUPS = [
+    (0, 2, False, "even"),
+    (2, 2, False, "odd"),
+    (4, 2, False, "even"),
+    (6, 1, True, "odd"),
+    (7, 1, True, "summed0"),
+]
+
+PLACES = [(0, 1), (0, 2), (0, 1), (1, 2)]
 
 
 def tile_picked_lnfold_silu_l_kernel(
@@ -32,9 +54,9 @@ def tile_picked_lnfold_silu_l_kernel(
         keep = ctx.enter_context(tc.tile_pool(name="keep", bufs=1))
         psum = ctx.enter_context(tc.psum_pool(name="psum", bufs=1))
 
-        offsets = keep.tile([P, S // 16], U16, name="offsets")
+        offsets = keep.tile([P, S // LIST_COLUMN], U16, name="offsets")
         stat_rows = keep.tile([2, T], F32, name="stat_rows")
-        stats = keep.tile([P, T], F32, name="stats", tag="window_then_picked", align_bytes=64)
+        stats = keep.tile([P, T], F32, name="stats")
         nc.vector.memset(stats[:].bitcast(I32), 0)
         warm = keep.tile([P, 2], F32, name="warm")
         nc.gpsimd.memset(warm[:, 0:1], 0.0)
@@ -44,25 +66,28 @@ def tile_picked_lnfold_silu_l_kernel(
         ident = keep.tile([P, P], F32, name="ident")
         make_identity(nc, ident[:])
 
-        rows = xT.rearrange("(p j) t -> p j t", j=4)
-        pairs = [keep.tile([P, 2 * T], BF16, name="pairs%d" % u, tag="pairs%d" % u, align_bytes=64) for u in range(2)]
-        raws = [keep.tile([P, 2, w], F32, name="raw%d" % i, tag="raw%d" % i) for i, (u, c0, w, v) in enumerate(LOADS)]
+        rows = xT.rearrange("(p t) c -> p t c", t=4)
+        pairs = [keep.tile([P, 2 * T], BF16, name="pair%d" % u, align_bytes=64) for u in range(2)]
+        raws = [
+            keep.tile([P, 2, width], F32, name="raw%d" % i, tag="raw%d" % i)
+            for i, (u, start, width, vector_cols) in enumerate(LOADS)
+        ]
         gsum_col = keep.tile([P, 1], F32, name="gsum_col")
         b_col = keep.tile([P, 1], F32, name="b_col")
         w_words = keep.tile([P, 2 * N], U8, name="w_words", align_bytes=64)
 
         def load(i):
-            u, c0, w, v = LOADS[i]
-            nc.sync.dma_start(out=raws[i][:], in_=rows[:, 2 * u : 2 * u + 2, c0 : c0 + w])
+            u, start, width, vector_cols = LOADS[i]
+            nc.sync.dma_start(out=raws[i][:], in_=rows[:, 2 * u : 2 * u + 2, start : start + width])
 
         def cast(i):
-            u, c0, w, v = LOADS[i]
-            dst = pairs[u][:, 2 * c0 : 2 * (c0 + w)].rearrange("p (t e) -> p t e", e=2)
-            src = raws[i][:].rearrange("p e t -> p t e")
-            if v > 0:
-                nc.vector.tensor_copy(out=dst[:, 0:v, :], in_=src[:, 0:v, :])
-            if v < w:
-                nc.scalar.copy(out=dst[:, v:w, :], in_=src[:, v:w, :])
+            u, start, width, vector_cols = LOADS[i]
+            dst = pairs[u][:, 2 * start : 2 * (start + width)].rearrange("p (c e) -> p c e", e=2)
+            src = raws[i][:].rearrange("p e c -> p c e")
+            if vector_cols > 0:
+                nc.vector.tensor_copy(out=dst[:, 0:vector_cols, :], in_=src[:, 0:vector_cols, :])
+            if vector_cols < width:
+                nc.scalar.copy(out=dst[:, vector_cols:width, :], in_=src[:, vector_cols:width, :])
 
         load(0)
         nc.sync.dma_start(out=stat_rows[0:1, :], in_=mean[0:1, :])
@@ -79,80 +104,99 @@ def tile_picked_lnfold_silu_l_kernel(
             )
         nc.sync.dma_start(out=b_col[:], in_=b)
 
-        gsum_turned = psum.tile([P, P], F32, name="gsum_turned", tag="g")
+        gsum_turned = psum.tile([P, P], F32, name="gsum_turned")
         nc.tensor.transpose(gsum_turned[:], gsum_col[:].to_broadcast([P, P]), ident[:])
-        gsum_row = keep.tile([P, P], F32, name="gsum_row")
-        nc.scalar.activation(out=gsum_row[:], in_=gsum_turned[:], func=ACT.Copy, scale=-1.0)
+        neg_gsum_row = keep.tile([P, P], F32, name="neg_gsum_row")
+        nc.scalar.activation(out=neg_gsum_row[:], in_=gsum_turned[:], func=ACT.Copy, scale=-1.0)
+
         nc.vector.tensor_copy(out=stats[0:2, :], in_=stat_rows[:])
         picked_stats = keep.tile([P, S], F32, name="picked_stats")
         nc.vector.tensor_copy(out=picked_stats[:], in_=stats[:].indirect(offsets[:]))
-        for i in range(len(LOADS)):
-            if LOADS[i][0] == 0:
-                cast(i)
+        for i in range(PAIR1_FIRST):
+            cast(i)
 
-        chunks = S // CHUNK
-        picks = keep.tile([P, 2 * S], U32, name="picks", tag="window_then_picked", align_bytes=64)
-        woven = [keep.tile([P, 2 * CHUNK], U32, name="woven%d" % c, align_bytes=64) for c in range(chunks)]
+        picks_odd = keep.tile([P, 4 * CHUNK], U32, name="picks_odd")
+        picks = [
+            keep.tile([P, 2 * CHUNK], U32, name="picks0"),
+            picks_odd,
+            keep.tile([P, 2 * CHUNK], U32, name="picks2"),
+            picks_odd,
+        ]
+        woven = [keep.tile([P, 2 * CHUNK], U32, name="woven%d" % c, align_bytes=64) for c in range(CHUNKS)]
 
-        def gather(u, c, width):
-            cols = slice(c // 16, (c + width) // 16)
+        def gather(u, c):
+            entries = slice(c * CHUNK // LIST_COLUMN, (c + 1) * CHUNK // LIST_COLUMN)
+            at = PLACES[c][u] * CHUNK
             nc.vector.tensor_copy(
-                out=picks[:, u * S + c : u * S + c + width], in_=pairs[u][:].bitcast(U32).indirect(offsets[:, cols])
+                out=picks[c][:, at : at + CHUNK], in_=pairs[u][:].bitcast(U32).indirect(offsets[:, entries])
             )
 
         def weave(c):
+            at = PLACES[c][0] * CHUNK
+            apart = (PLACES[c][1] - PLACES[c][0]) * CHUNK
             dst = woven[c][:].rearrange("p (j u) -> p j u", u=2)
-            src = picks[:].rearrange("p (u j) -> p j u", u=2)[:, c * CHUNK : (c + 1) * CHUNK, :]
-            nc.vector.tensor_copy(out=dst.bitcast(I32), in_=src.bitcast(I32))
+            src = picks[c][:, at : at + 2 * apart].rearrange("p (u j) -> p j u", u=2)[:, 0:CHUNK, :]
+            if c < CHUNKS - 1:
+                nc.scalar.copy(out=dst, in_=src)
+            else:
+                nc.vector.tensor_copy(out=dst.bitcast(I32), in_=src.bitcast(I32))
 
-        gather(0, 0, S)
-        token_stats = keep.tile([P, BLOCKS, 2], F32, name="token_stats", tag="pairs0", align_bytes=64)
-        for h in range(2):
-            turned = psum.tile([P, 4, P], F32, name="turned%d" % h, tag="ab"[h])
-            for i in range(4):
-                blk = 4 * h + i
+        for c in range(CHUNKS):
+            gather(0, c)
+        cast(PAIR1_FIRST)
+
+        token_stats = keep.tile([P, BLOCKS, 2], F32, name="token_stats", tag="raw%d" % PAIR1_FIRST)
+        for h, bank in enumerate(("even", "odd")):
+            turned = psum.tile([P, BLOCKS_A_BANK, P], F32, name="turned%d" % h, tag=bank)
+            first = BLOCKS_A_BANK * h
+            for i in range(BLOCKS_A_BANK):
+                blk = first + i
                 nc.tensor.transpose(turned[:, i, :], picked_stats[:, blk * P : (blk + 1) * P], ident[:])
-            nc.vector.tensor_copy(out=token_stats[:, 4 * h : 4 * h + 4, :], in_=turned[:, :, 0:2])
-        shift = keep.tile([P, BLOCKS], F32, name="shift")
-        nc.vector.tensor_tensor(out=shift[:], in0=token_stats[:, :, 0], in1=token_stats[:, :, 1], op=ALU.mult)
-        for i in range(len(LOADS)):
-            if LOADS[i][0] == 1:
-                cast(i)
+            nc.scalar.copy(out=token_stats[:, first : first + BLOCKS_A_BANK, :], in_=turned[:, :, 0:2])
+        mean_inv = keep.tile([P, BLOCKS], F32, name="mean_inv")
+        nc.vector.tensor_tensor(out=mean_inv[:], in0=token_stats[:, :, 0], in1=token_stats[:, :, 1], op=ALU.mult)
+        for i in range(PAIR1_FIRST + 1, len(LOADS)):
+            cast(i)
 
-        correction = keep.tile([P, BLOCKS, N], F32, name="correction", tag="raw%d" % (len(LOADS) - 1))
+        correction = keep.tile([P, BLOCKS, N], F32, name="correction", tag="raw%d" % (PAIR1_FIRST + 1))
         for blk in range(BLOCKS):
             nc.scalar.activation(
-                out=correction[:, blk, :], in_=gsum_row[:], func=ACT.Copy, scale=shift[:, blk : blk + 1]
+                out=correction[:, blk, :], in_=neg_gsum_row[:], func=ACT.Copy, scale=mean_inv[:, blk : blk + 1]
             )
-        zs = []
-        for n, (first, count, on_vector, bank) in enumerate(UNITS):
-            zs.append(psum.tile([P, count, P], F32, name="z%d" % n))
+
+        summed = []
+        for n, (first, count, on_vector, bank) in enumerate(GROUPS):
+            summed.append(psum.tile([P, count, P], F32, name="summed%d" % n, tag="summed%d" % n))
             if not on_vector:
                 for i in range(count):
                     nc.tensor.matmul(
-                        zs[n][:, i, :], correction[:, first + i, :], ident[:],
+                        summed[n][:, i, :], correction[:, first + i, :], ident[:],
                         start=(i == 0), stop=False, is_transpose=True,
                     )
 
-        results = []
-
         def finish(n):
-            first, count, on_vector, bank = UNITS[n]
+            first, count, on_vector, bank = GROUPS[n]
             width = count * P
+            c, inside = divmod(first * P, CHUNK)
             codes = keep.tile([P, width], U32, name="codes%d" % n, align_bytes=64)
             scales = keep.tile([P, width], U8, name="scales%d" % n, align_bytes=64)
             nc.vector.quantize_mx(
-                out=codes[:].bitcast(FP8X4), scales=scales[:],
-                in_=woven[first * P // CHUNK][:, 2 * (first * P % CHUNK) : 2 * (first * P % CHUNK + width)].bitcast(BF16),
+                out=codes[:].bitcast(FP8X4),
+                scales=scales[:],
+                in_=woven[c][:, 2 * inside : 2 * (inside + width)].bitcast(BF16),
             )
             y = psum.tile([P, count, N], F32, name="y%d" % n, tag=bank)
-            z = zs[n]
             scaled = keep.tile([P, count, N], F32, name="scaled%d" % n)
             for i in range(count):
-                cols = slice(i * P, (i + 1) * P)
+                tokens = slice(i * P, (i + 1) * P)
                 nc.tensor.matmul_mx(
-                    out=y[:, i, :], lhsT=codes[:, cols].bitcast(FP8X4), lhsT_scale=scales[:, cols],
-                    rhs=w_words[:].bitcast(FP4X4), rhs_scale=w_scales[:], start=True, stop=True,
+                    out=y[:, i, :],
+                    lhsT=codes[:, tokens].bitcast(FP8X4),
+                    lhsT_scale=scales[:, tokens],
+                    rhs=w_words[:].bitcast(FP4X4),
+                    rhs_scale=w_scales[:],
+                    start=True,
+                    stop=True,
                 )
             for i in range(count):
                 blk = first + i
@@ -167,27 +211,26 @@ def tile_picked_lnfold_silu_l_kernel(
                     )
             for i in range(count):
                 nc.tensor.matmul(
-                    z[:, i, :], scaled[:, i, :], ident[:],
-                    start=on_vector, stop=(on_vector or i == count - 1), is_transpose=True,
+                    summed[n][:, i, :], scaled[:, i, :], ident[:],
+                    start=on_vector, stop=(i == count - 1), is_transpose=True,
                 )
             result = keep.tile([P, count, P], F32, name="result%d" % n)
-            results.append(result)
-            nc.scalar.activation(out=result[:], in_=z[:], func=ACT.Silu, bias=b_col[:])
-            queue = nc.scalar if n == len(UNITS) - 1 else nc.sync
+            nc.scalar.activation(out=result[:], in_=summed[n][:], func=ACT.Silu, bias=b_col[:])
+            queue = nc.scalar if n == len(GROUPS) - 1 else nc.sync
             queue.dma_start(
                 out=out[:, first * P : first * P + width], in_=result[:].rearrange("p i j -> p (i j)")
             )
 
-        gather(1, 0, CHUNK)
-        gather(1, CHUNK, CHUNK)
+        gather(1, 0)
+        gather(1, 1)
         weave(0)
-        gather(1, 2 * CHUNK, CHUNK)
-        finish(0)
         weave(1)
-        gather(1, 3 * CHUNK, CHUNK)
-        finish(1)
+        gather(1, 2)
         weave(2)
-        weave(3)
+        finish(0)
+        finish(1)
+        gather(1, 3)
         finish(2)
+        weave(3)
         finish(3)
         finish(4)

from contextlib import ExitStack

import concourse.mybir as mybir
from concourse.masks import make_identity

K, T, S, N = 512, 2048, 1024, 128
P = 128
FLOPS = 2 * K * S * N

F32 = mybir.dt.float32
BF16 = mybir.dt.bfloat16
I32 = mybir.dt.int32
U32 = mybir.dt.uint32
U16 = mybir.dt.uint16
U8 = mybir.dt.uint8
FP8X4 = mybir.dt.float8_e4m3fn_x4
FP4X4 = mybir.dt.float4_e2m1fn_x4
ACT = mybir.ActivationFunctionType
ALU = mybir.AluOpType

LIST_COLUMN = 16
CHUNK = 256
CHUNKS = S // CHUNK
BLOCKS = S // P
BLOCKS_A_BANK = 4

LOADS = [
    (0, 0, 256, 0),
    (0, 256, 768, 0),
    (0, 1024, 1024, 704),
    (1, 0, 512, 0),
    (1, 512, 512, 0),
    (1, 1024, 640, 640),
    (1, 1664, 384, 384),
]
PAIR1_FIRST = 3

GROUPS = [
    (0, 2, False, "even"),
    (2, 2, False, "odd"),
    (4, 2, False, "even"),
    (6, 1, True, "odd"),
    (7, 1, True, "summed0"),
]

PLACES = [(0, 1), (0, 2), (0, 1), (1, 2)]


def tile_picked_lnfold_silu_l_kernel(
    tc, xT, mean, inv, gsum, b, w1_words, w1_scales, offs, out
):
    nc = tc.nc
    with ExitStack() as ctx:
        keep = ctx.enter_context(tc.tile_pool(name="keep", bufs=1))
        psum = ctx.enter_context(tc.psum_pool(name="psum", bufs=1))

        offsets = keep.tile([P, S // LIST_COLUMN], U16, name="offsets")
        stat_rows = keep.tile([2, T], F32, name="stat_rows")
        stats = keep.tile([P, T], F32, name="stats")
        nc.vector.memset(stats[:].bitcast(I32), 0)
        warm = keep.tile([P, 2], F32, name="warm")
        nc.gpsimd.memset(warm[:, 0:1], 0.0)
        nc.scalar.activation(out=warm[:, 1:2], in_=warm[:, 0:1], func=ACT.Silu)
        w_scales = keep.tile([P, N], U8, name="w_scales", align_bytes=64)
        nc.gpsimd.memset(w_scales[:], 0)
        ident = keep.tile([P, P], F32, name="ident")
        make_identity(nc, ident[:])

        rows = xT.rearrange("(p t) c -> p t c", t=4)
        pairs = [keep.tile([P, 2 * T], BF16, name="pair%d" % u, align_bytes=64) for u in range(2)]
        raws = [
            keep.tile([P, 2, width], F32, name="raw%d" % i, tag="raw%d" % i)
            for i, (u, start, width, vector_cols) in enumerate(LOADS)
        ]
        gsum_col = keep.tile([P, 1], F32, name="gsum_col")
        b_col = keep.tile([P, 1], F32, name="b_col")
        w_words = keep.tile([P, 2 * N], U8, name="w_words", align_bytes=64)

        def load(i):
            u, start, width, vector_cols = LOADS[i]
            nc.sync.dma_start(out=raws[i][:], in_=rows[:, 2 * u : 2 * u + 2, start : start + width])

        def cast(i):
            u, start, width, vector_cols = LOADS[i]
            dst = pairs[u][:, 2 * start : 2 * (start + width)].rearrange("p (c e) -> p c e", e=2)
            src = raws[i][:].rearrange("p e c -> p c e")
            if vector_cols > 0:
                nc.vector.tensor_copy(out=dst[:, 0:vector_cols, :], in_=src[:, 0:vector_cols, :])
            if vector_cols < width:
                nc.scalar.copy(out=dst[:, vector_cols:width, :], in_=src[:, vector_cols:width, :])

        load(0)
        nc.sync.dma_start(out=stat_rows[0:1, :], in_=mean[0:1, :])
        nc.sync.dma_start(out=stat_rows[1:2, :], in_=inv[0:1, :])
        nc.sync.dma_start(offsets[:], offs)
        nc.sync.dma_start(out=gsum_col[:], in_=gsum)
        for i in range(1, len(LOADS)):
            load(i)
        nc.sync.dma_start(out=w_words[:], in_=w1_words[0])
        for q in range(4):
            nc.sync.dma_start(
                out=w_scales[32 * q : 32 * q + 4, :].bitcast(I32),
                in_=w1_scales[0, 4 * q : 4 * q + 4, :].bitcast(I32),
            )
        nc.sync.dma_start(out=b_col[:], in_=b)

        gsum_turned = psum.tile([P, P], F32, name="gsum_turned")
        nc.tensor.transpose(gsum_turned[:], gsum_col[:].to_broadcast([P, P]), ident[:])
        neg_gsum_row = keep.tile([P, P], F32, name="neg_gsum_row")
        nc.scalar.activation(out=neg_gsum_row[:], in_=gsum_turned[:], func=ACT.Copy, scale=-1.0)

        nc.vector.tensor_copy(out=stats[0:2, :], in_=stat_rows[:])
        picked_stats = keep.tile([P, S], F32, name="picked_stats")
        nc.vector.tensor_copy(out=picked_stats[:], in_=stats[:].indirect(offsets[:]))
        for i in range(PAIR1_FIRST):
            cast(i)

        picks_odd = keep.tile([P, 4 * CHUNK], U32, name="picks_odd")
        picks = [
            keep.tile([P, 2 * CHUNK], U32, name="picks0"),
            picks_odd,
            keep.tile([P, 2 * CHUNK], U32, name="picks2"),
            picks_odd,
        ]
        woven = [keep.tile([P, 2 * CHUNK], U32, name="woven%d" % c, align_bytes=64) for c in range(CHUNKS)]

        def gather(u, c):
            entries = slice(c * CHUNK // LIST_COLUMN, (c + 1) * CHUNK // LIST_COLUMN)
            at = PLACES[c][u] * CHUNK
            nc.vector.tensor_copy(
                out=picks[c][:, at : at + CHUNK], in_=pairs[u][:].bitcast(U32).indirect(offsets[:, entries])
            )

        def weave(c):
            at = PLACES[c][0] * CHUNK
            apart = (PLACES[c][1] - PLACES[c][0]) * CHUNK
            dst = woven[c][:].rearrange("p (j u) -> p j u", u=2)
            src = picks[c][:, at : at + 2 * apart].rearrange("p (u j) -> p j u", u=2)[:, 0:CHUNK, :]
            if c < CHUNKS - 1:
                nc.scalar.copy(out=dst, in_=src)
            else:
                nc.vector.tensor_copy(out=dst.bitcast(I32), in_=src.bitcast(I32))

        for c in range(CHUNKS):
            gather(0, c)
        cast(PAIR1_FIRST)

        token_stats = keep.tile([P, BLOCKS, 2], F32, name="token_stats", tag="raw%d" % PAIR1_FIRST)
        for h, bank in enumerate(("even", "odd")):
            turned = psum.tile([P, BLOCKS_A_BANK, P], F32, name="turned%d" % h, tag=bank)
            first = BLOCKS_A_BANK * h
            for i in range(BLOCKS_A_BANK):
                blk = first + i
                nc.tensor.transpose(turned[:, i, :], picked_stats[:, blk * P : (blk + 1) * P], ident[:])
            nc.scalar.copy(out=token_stats[:, first : first + BLOCKS_A_BANK, :], in_=turned[:, :, 0:2])
        mean_inv = keep.tile([P, BLOCKS], F32, name="mean_inv")
        nc.vector.tensor_tensor(out=mean_inv[:], in0=token_stats[:, :, 0], in1=token_stats[:, :, 1], op=ALU.mult)
        for i in range(PAIR1_FIRST + 1, len(LOADS)):
            cast(i)

        correction = keep.tile([P, BLOCKS, N], F32, name="correction", tag="raw%d" % (PAIR1_FIRST + 1))
        for blk in range(BLOCKS):
            nc.scalar.activation(
                out=correction[:, blk, :], in_=neg_gsum_row[:], func=ACT.Copy, scale=mean_inv[:, blk : blk + 1]
            )

        summed = []
        for n, (first, count, on_vector, bank) in enumerate(GROUPS):
            summed.append(psum.tile([P, count, P], F32, name="summed%d" % n, tag="summed%d" % n))
            if not on_vector:
                for i in range(count):
                    nc.tensor.matmul(
                        summed[n][:, i, :], correction[:, first + i, :], ident[:],
                        start=(i == 0), stop=False, is_transpose=True,
                    )

        def finish(n):
            first, count, on_vector, bank = GROUPS[n]
            width = count * P
            c, inside = divmod(first * P, CHUNK)
            codes = keep.tile([P, width], U32, name="codes%d" % n, align_bytes=64)
            scales = keep.tile([P, width], U8, name="scales%d" % n, align_bytes=64)
            nc.vector.quantize_mx(
                out=codes[:].bitcast(FP8X4),
                scales=scales[:],
                in_=woven[c][:, 2 * inside : 2 * (inside + width)].bitcast(BF16),
            )
            y = psum.tile([P, count, N], F32, name="y%d" % n, tag=bank)
            scaled = keep.tile([P, count, N], F32, name="scaled%d" % n)
            for i in range(count):
                tokens = slice(i * P, (i + 1) * P)
                nc.tensor.matmul_mx(
                    out=y[:, i, :],
                    lhsT=codes[:, tokens].bitcast(FP8X4),
                    lhsT_scale=scales[:, tokens],
                    rhs=w_words[:].bitcast(FP4X4),
                    rhs_scale=w_scales[:],
                    start=True,
                    stop=True,
                )
            for i in range(count):
                blk = first + i
                if on_vector:
                    nc.vector.scalar_tensor_tensor(
                        out=scaled[:, i, :], in0=y[:, i, :], scalar=token_stats[:, blk, 1:2],
                        in1=correction[:, blk, :], op0=ALU.mult, op1=ALU.add,
                    )
                else:
                    nc.scalar.activation(
                        out=scaled[:, i, :], in_=y[:, i, :], func=ACT.Copy, scale=token_stats[:, blk, 1:2]
                    )
            for i in range(count):
                nc.tensor.matmul(
                    summed[n][:, i, :], scaled[:, i, :], ident[:],
                    start=on_vector, stop=(i == count - 1), is_transpose=True,
                )
            result = keep.tile([P, count, P], F32, name="result%d" % n)
            nc.scalar.activation(out=result[:], in_=summed[n][:], func=ACT.Silu, bias=b_col[:])
            queue = nc.scalar if n == len(GROUPS) - 1 else nc.sync
            queue.dma_start(
                out=out[:, first * P : first * P + width], in_=result[:].rearrange("p i j -> p (i j)")
            )

        gather(1, 0)
        gather(1, 1)
        weave(0)
        weave(1)
        gather(1, 2)
        weave(2)
        finish(0)
        finish(1)
        gather(1, 3)
        finish(2)
        weave(3)
        finish(3)
        finish(4)
